import numpy as np
import ml_dtypes


def mxq(x, axis, fmt="e4m3"):
    dtype, down = {"e4m3": (ml_dtypes.float8_e4m3fn, 7), "e5m2": (ml_dtypes.float8_e5m2, 14)}[fmt]
    v = np.moveaxis(np.asarray(x, np.float32).astype(ml_dtypes.bfloat16).astype(np.float64), axis, -1)
    blocks = v.reshape(v.shape[:-1] + (-1, 32))
    amax = np.abs(blocks).max(-1, keepdims=True)
    byte = np.maximum(np.where(amax > 0, np.frexp(amax)[1] - 1 + 127, 0) - down, 1)
    scale = np.exp2(byte - 127.0)
    codes = (blocks / scale).astype(np.float32).astype(dtype).astype(np.float64)
    return np.moveaxis((codes * scale).reshape(v.shape), -1, axis)


WIDE = False


def mx_kscale(k):
    if not WIDE:
        return np.ones(k)
    levels = np.array([30, -30])
    if k % 512:
        return np.exp2(np.random.permutation(np.resize(levels, k // 32))).repeat(32)
    a = np.empty((k // 512, 16))
    for p in range(k // 512):
        a[p, :8] = np.random.permutation(np.resize(levels, 8))
        for g in range(8):
            far = levels[np.abs(levels - a[p, g]) >= 10]
            a[p, g + 8] = far[np.random.randint(len(far))]
    return np.exp2(a.ravel()).repeat(32)


def f64(x):
    return np.asarray(x).astype(np.float64)


def striped(idx):
    return np.tile(np.asarray(idx).reshape(-1, 16).T, (8, 1)).astype(np.uint16)


def unstriped(offs):
    return offs[:16].T.reshape(-1).astype(np.int64)


E2M1 = np.array([0.0, 0.5, 1.0, 1.5, 2.0, 3.0, 4.0, 6.0, -0.0, -0.5, -1.0, -1.5, -2.0, -3.0, -4.0, -6.0])


def pack_weight(w, fmt):
    k, n = w.shape
    w = f64(np.asarray(w, np.float32).astype(ml_dtypes.bfloat16)).reshape(k // 32, 32, n)
    amax = np.abs(w).max(1)
    if fmt == "e4m3":
        byte = np.frexp(amax)[1] - 1 + 127 - 7
    else:
        mant, ex = np.frexp(amax / 6.0)
        byte = np.where(mant > 0.5, ex, ex - 1) + 127
    byte = np.clip(np.where(amax > 0, byte, 1), 1, 254)
    scaled = (w * np.exp2(127.0 - byte)[:, None, :]).reshape(k, n).astype(np.float32)
    by_word = np.ascontiguousarray(scaled.reshape(k // 512, 128, 4, n).transpose(0, 1, 3, 2))
    if fmt == "e4m3":
        words = by_word.astype(ml_dtypes.float8_e4m3fn).view(np.uint8)
    else:
        c = by_word.astype(ml_dtypes.float4_e2m1fn).view(np.uint8) & 0xF
        words = (c[..., 0::2] | (c[..., 1::2] << 4)).reshape(k // 512, 128, 2 * n)
    return np.ascontiguousarray(words), np.ascontiguousarray(byte.astype(np.uint8).reshape(k // 512, 16, n))


def unpack_weight(words, scales, fmt):
    g, _, n = scales.shape
    words = np.ascontiguousarray(words).reshape(g, 128, n, -1)
    if fmt == "e4m3":
        vals = words.view(ml_dtypes.float8_e4m3fn).astype(np.float64)
    else:
        nib = np.empty((g, 128, n, 4), np.uint8)
        nib[..., 0::2] = words & 0xF
        nib[..., 1::2] = words >> 4
        vals = E2M1[nib]
    vals = vals * np.repeat(np.exp2(scales.astype(np.float64) - 127.0), 8, axis=1)[..., None]
    return vals.transpose(0, 1, 3, 2).reshape(g * 512, n)


K, T, J, R, N = 512, 1024, 256, 512, 256


def setup_inputs():
    n = np.random.standard_normal
    idx = np.random.permutation(T)[:J]
    idx2 = np.random.permutation(T)[:J]
    fk = mx_kscale(K)
    fr = mx_kscale(R)
    wbp = pack_weight(n((R, N)) * 1 / np.sqrt(R) / fr[:, None], "e2m1")
    return {
        "xf": (n((K, T))).astype(np.float32),
        "fk": (np.random.uniform(0.5, 2.0, (K, 1)) / fk[:, None]).astype(np.float32),
        "w": (n((K, R)) * 1 / np.sqrt(K) * fk[:, None] * fr).astype(np.float32),
        "wb_words": wbp[0],
        "wb_scales": wbp[1],
        "rs": (n((N, J))).astype(np.float32),
        "offs": striped(idx),
        "offs2": striped(idx2),
    }


def reference(xf, fk, w, wb_words, wb_scales, rs, offs, offs2):
    idx = unstriped(offs)
    idx2 = unstriped(offs2)
    wbu = unpack_weight(wb_words, wb_scales, "e2m1")
    u = np.maximum(f64(xf)[:, idx], f64(xf)[:, idx2]) * f64(fk)
    wq = mxq(f64(w), 0, "e5m2")
    uq = mxq(u, 0, "e4m3")
    a = wq.T @ uq
    ha = np.maximum(a, 0.0)
    h1 = np.pad(ha, ((0, 0), (2, 0)))[:, :J]
    hid = ha - 0.5 * h1
    hidq = mxq(hid, 0, "e5m2")
    p = wbu.T @ hidq
    p1 = np.pad(p, ((0, 0), (1, 0)))[:, :J]
    y = p - 0.7 * p1 + 0.5 * f64(rs)
    return y

@@ -1,0 +1,195 @@
+from contextlib import ExitStack
+
+import concourse.mybir as mybir
+
+K, T, J, R, N = 512, 1024, 256, 512, 256
+FLOPS = 2 * K * R * J + 2 * R * N * J
+
+F32 = mybir.dt.float32
+BF16 = mybir.dt.bfloat16
+I32 = mybir.dt.int32
+U32 = mybir.dt.uint32
+U16 = mybir.dt.uint16
+U8 = mybir.dt.uint8
+E4M3 = mybir.dt.float8_e4m3fn_x4
+E5M2 = mybir.dt.float8_e5m2_x4
+E2M1 = mybir.dt.float4_e2m1fn_x4
+ALU = mybir.AluOpType
+ACT = mybir.ActivationFunctionType
+
+P = 128
+PACK = 4
+HALF_J = J // 2
+HALF_M = P // 2
+LAG = 2
+SCALAR_SHARE = (64, 40)
+
+
+def tile_list_largerpicks_lagged_lagged_kernel(tc, xf, fk, w, wb_words, wb_scales, rs, offs, offs2, out):
+    nc = tc.nc
+    with ExitStack() as ctx:
+        keep = ctx.enter_context(tc.tile_pool(name="keep", bufs=1))
+        psum = ctx.enter_context(tc.psum_pool(name="psum", bufs=1))
+
+        list_a = keep.tile([P, J // 16], U16, name="list_a")
+        list_b = keep.tile([P, J // 16], U16, name="list_b")
+        x_rows = [keep.tile([P, T], F32, name="x_rows%d" % i, tag="x%d" % i, align_bytes=64) for i in range(PACK)]
+        w_raw = [keep.tile([P, PACK, R // 2], F32, name="w_raw%d" % h) for h in range(2)]
+        factor = [keep.tile([P, 2], F32, name="factor%d" % h) for h in range(2)]
+        wb_codes = keep.tile([P, 2 * N], U8, name="wb_codes", align_bytes=64)
+        wb_plane = keep.tile([P, N], U8, name="wb_plane", align_bytes=64)
+        resid = keep.tile([P, 2, J], F32, name="resid")
+        relu = keep.tile([P, PACK * (LAG + J)], F32, name="relu")
+
+        nc.gpsimd.memset(wb_plane[:].bitcast(U32), 0)
+        nc.vector.memset(relu[:, 0 : PACK * LAG], 0.0)
+
+        xv = xf.rearrange("(p i) t -> p i t", i=PACK)
+        wv = w.rearrange("(p i) r -> p i r", i=PACK)
+        nc.sync.dma_start(out=x_rows[0][:], in_=xv[:, 0, :])
+        nc.sync.dma_start(list_a[:], offs)
+        nc.sync.dma_start(list_b[:], offs2)
+        fv = fk.rearrange("(p i) o -> p (i o)", i=PACK)
+        for i in range(1, PACK):
+            nc.sync.dma_start(out=x_rows[i][:], in_=xv[:, i, :])
+            if i >= 2:
+                nc.sync.dma_start(out=factor[i - 2][:], in_=fv[:, 2 * (i - 2) : 2 * (i - 1)])
+        for h in range(2):
+            nc.sync.dma_start(out=w_raw[h][:], in_=wv[:, :, h * (R // 2) : (h + 1) * (R // 2)])
+        nc.sync.dma_start(out=wb_codes[:].bitcast(I32), in_=wb_words[0].bitcast(I32))
+        for q in range(4):
+            nc.sync.dma_start(
+                out=wb_plane[32 * q : 32 * q + 4, :].bitcast(I32),
+                in_=wb_scales[0, 4 * q : 4 * q + 4, :].bitcast(I32),
+            )
+        nc.sync.dma_start(out=resid[:], in_=rs.rearrange("(c p) j -> p c j", p=P))
+
+        larger = [keep.tile([P, J], F32, name="larger%d" % i) for i in range(PACK)]
+        pick_a = [keep.tile([P, J], F32, name="pick_a%d" % i) for i in range(PACK)]
+        pick_b = [keep.tile([P, J], F32, name="pick_b%d" % i) for i in range(PACK)]
+
+        def gather(i):
+            nc.scalar.activation(pick_a[i][:], x_rows[i][:].indirect(list_a[:]), ACT.Copy)
+            nc.vector.tensor_copy(pick_b[i][:], x_rows[i][:].indirect(list_b[:]))
+
+        def keep_larger(i):
+            nc.vector.tensor_tensor(larger[i][:], pick_a[i][:], pick_b[i][:], ALU.max)
+
+        early = keep.tile([P, PACK - 1, J], BF16, name="early")
+
+        def scale(i, dest):
+            nc.vector.tensor_scalar(dest, larger[i][:], factor[i // 2][:, i % 2 : i % 2 + 1], None, ALU.mult)
+
+        for i in range(2):
+            gather(i)
+            keep_larger(i)
+        gather(2)
+        scale(0, early[:, 0, :])
+        scale(1, early[:, 1, :])
+        keep_larger(2)
+        gather(3)
+        scale(2, early[:, 2, :])
+        keep_larger(3)
+        u_bf = keep.tile([P, J, PACK], BF16, name="u_bf", tag="x3", align_bytes=64)
+        nc.vector.tensor_copy(u_bf[:, :, 0 : PACK - 1], early[:].rearrange("p i j -> p j i"))
+        scale(3, u_bf[:, :, 3])
+
+        u_codes = keep.tile([P, J], U32, name="u_codes", align_bytes=64)
+        u_plane = keep.tile([P, J], U8, name="u_plane", align_bytes=64)
+        nc.vector.quantize_mx(
+            out=u_codes[:].bitcast(E4M3), scales=u_plane[:], in_=u_bf[:].rearrange("p j i -> p (j i)")
+        )
+
+        w_codes = keep.tile([P, R], U32, name="w_codes", align_bytes=64)
+        w_plane = keep.tile([P, R], U8, name="w_plane", align_bytes=64)
+        w_bf = [keep.tile([P, PACK, HALF_M, PACK], BF16, name="w_bf%d" % h, align_bytes=64) for h in range(2)]
+        for h in range(2):
+            dealt = w_bf[h][:].rearrange("p t m i -> p m t i")
+            source = w_raw[h][:].rearrange("p i (m t) -> p m t i", t=PACK)
+            cut = SCALAR_SHARE[h]
+            nc.scalar.copy(dealt[:, 0:cut], source[:, 0:cut])
+            if cut < HALF_M:
+                nc.vector.tensor_copy(dealt[:, cut:HALF_M], source[:, cut:HALF_M])
+        for h in range(2):
+            for t in range(PACK):
+                cols = slice(t * P + h * HALF_M, t * P + (h + 1) * HALF_M)
+                nc.vector.quantize_mx(
+                    out=w_codes[:, cols].bitcast(E5M2),
+                    scales=w_plane[:, cols],
+                    in_=w_bf[h][:, t].rearrange("p m i -> p (m i)"),
+                )
+
+        first = [psum.tile([P, PACK, HALF_J], F32, name="first%d" % s) for s in range(2)]
+        for s in range(2):
+            slots = slice(s * HALF_J, (s + 1) * HALF_J)
+            for t in range(PACK):
+                cols = slice(t * P, (t + 1) * P)
+                nc.tensor.matmul_mx(
+                    out=first[s][:, t, :],
+                    lhsT=w_codes[:, cols].bitcast(E5M2),
+                    lhsT_scale=w_plane[:, cols],
+                    rhs=u_codes[:, slots].bitcast(E4M3),
+                    rhs_scale=u_plane[:, slots],
+                    start=True,
+                    stop=True,
+                )
+
+        hid_bf = [keep.tile([P, PACK * HALF_J], BF16, name="hid_bf%d" % s, align_bytes=64) for s in range(2)]
+        hid_codes = [keep.tile([P, HALF_J], U32, name="hid_codes%d" % s, align_bytes=64) for s in range(2)]
+        hid_plane = [keep.tile([P, HALF_J], U8, name="hid_plane%d" % s, align_bytes=64) for s in range(2)]
+        second = [[psum.tile([P, HALF_J], F32, name="second%d%d" % (s, c)) for c in range(2)] for s in range(2)]
+        quarter = HALF_J // 2
+
+        def hidden(s, e):
+            j0 = s * HALF_J + e * quarter
+            now = relu[:, PACK * (LAG + j0) : PACK * (LAG + j0 + quarter)]
+            before = relu[:, PACK * j0 : PACK * (j0 + quarter)]
+            nc.scalar.activation(
+                now.rearrange("p (j t) -> p j t", t=PACK),
+                first[s][:, :, e * quarter : (e + 1) * quarter].rearrange("p t j -> p j t"),
+                ACT.Relu,
+            )
+            nc.vector.scalar_tensor_tensor(
+                hid_bf[s][:, PACK * e * quarter : PACK * (e + 1) * quarter], before, -0.5, now, ALU.mult, ALU.add
+            )
+
+        def second_product(s):
+            nc.vector.quantize_mx(out=hid_codes[s][:].bitcast(E5M2), scales=hid_plane[s][:], in_=hid_bf[s][:])
+            for c in range(2):
+                nc.tensor.matmul_mx(
+                    out=second[s][c][:],
+                    lhsT=wb_codes[:, 2 * P * c : 2 * P * (c + 1)].bitcast(E2M1),
+                    lhsT_scale=wb_plane[:, P * c : P * (c + 1)],
+                    rhs=hid_codes[s][:].bitcast(E5M2),
+                    rhs_scale=hid_plane[s][:],
+                    start=True,
+                    stop=True,
+                )
+
+        hidden(0, 0)
+        hidden(0, 1)
+        hidden(1, 0)
+        second_product(0)
+        hidden(1, 1)
+        second_product(1)
+
+        out_v = out.rearrange("(c p) j -> p c j", p=P)
+        for s in range(2):
+            j0 = s * HALF_J
+            lagged = min(HALF_J, J - 1 - j0)
+            result = [keep.tile([P, HALF_J], F32, name="result%d%d" % (s, c)) for c in range(2)]
+            for c in range(2):
+                nc.vector.scalar_tensor_tensor(
+                    resid[:, c, j0 + 1 : j0 + 1 + lagged],
+                    second[s][c][:, 0:lagged],
+                    -1.4,
+                    resid[:, c, j0 + 1 : j0 + 1 + lagged],
+                    ALU.mult,
+                    ALU.add,
+                )
+            for c in range(2):
+                nc.vector.scalar_tensor_tensor(
+                    result[c][:], resid[:, c, j0 : j0 + HALF_J], 0.5, second[s][c][:], ALU.mult, ALU.add
+                )
+                queue = nc.sync if c == 0 else nc.scalar
+                queue.dma_start(out=out_v[:, c, j0 : j0 + HALF_J], in_=result[c][:])

@@ -43,6 +43,8 @@ def tile_list_largerpicks_lagged_lagged_kernel(tc, xf, fk, w, wb_words, wb_scale
 
         nc.gpsimd.memset(wb_plane[:].bitcast(U32), 0)
         nc.vector.memset(relu[:, 0 : PACK * LAG], 0.0)
+        warm = keep.tile([P, 1], F32, name="warm")
+        nc.scalar.activation(warm[:], relu[:, 0:1], ACT.Relu)
 
         xv = xf.rearrange("(p i) t -> p i t", i=PACK)
         wv = w.rearrange("(p i) r -> p i r", i=PACK)

from contextlib import ExitStack

import concourse.mybir as mybir

K, T, J, R, N = 512, 1024, 256, 512, 256
FLOPS = 2 * K * R * J + 2 * R * N * J

F32 = mybir.dt.float32
BF16 = mybir.dt.bfloat16
I32 = mybir.dt.int32
U32 = mybir.dt.uint32
U16 = mybir.dt.uint16
U8 = mybir.dt.uint8
E4M3 = mybir.dt.float8_e4m3fn_x4
E5M2 = mybir.dt.float8_e5m2_x4
E2M1 = mybir.dt.float4_e2m1fn_x4
ALU = mybir.AluOpType
ACT = mybir.ActivationFunctionType

P = 128
PACK = 4
HALF_J = J // 2
HALF_M = P // 2
LAG = 2
SCALAR_SHARE = (64, 40)


def tile_list_largerpicks_lagged_lagged_kernel(tc, xf, fk, w, wb_words, wb_scales, rs, offs, offs2, out):
    nc = tc.nc
    with ExitStack() as ctx:
        keep = ctx.enter_context(tc.tile_pool(name="keep", bufs=1))
        psum = ctx.enter_context(tc.psum_pool(name="psum", bufs=1))

        list_a = keep.tile([P, J // 16], U16, name="list_a")
        list_b = keep.tile([P, J // 16], U16, name="list_b")
        x_rows = [keep.tile([P, T], F32, name="x_rows%d" % i, tag="x%d" % i, align_bytes=64) for i in range(PACK)]
        w_raw = [keep.tile([P, PACK, R // 2], F32, name="w_raw%d" % h) for h in range(2)]
        factor = [keep.tile([P, 2], F32, name="factor%d" % h) for h in range(2)]
        wb_codes = keep.tile([P, 2 * N], U8, name="wb_codes", align_bytes=64)
        wb_plane = keep.tile([P, N], U8, name="wb_plane", align_bytes=64)
        resid = keep.tile([P, 2, J], F32, name="resid")
        relu = keep.tile([P, PACK * (LAG + J)], F32, name="relu")

        nc.gpsimd.memset(wb_plane[:].bitcast(U32), 0)
        nc.vector.memset(relu[:, 0 : PACK * LAG], 0.0)
        warm = keep.tile([P, 1], F32, name="warm")
        nc.scalar.activation(warm[:], relu[:, 0:1], ACT.Relu)

        xv = xf.rearrange("(p i) t -> p i t", i=PACK)
        wv = w.rearrange("(p i) r -> p i r", i=PACK)
        nc.sync.dma_start(out=x_rows[0][:], in_=xv[:, 0, :])
        nc.sync.dma_start(list_a[:], offs)
        nc.sync.dma_start(list_b[:], offs2)
        fv = fk.rearrange("(p i) o -> p (i o)", i=PACK)
        for i in range(1, PACK):
            nc.sync.dma_start(out=x_rows[i][:], in_=xv[:, i, :])
            if i >= 2:
                nc.sync.dma_start(out=factor[i - 2][:], in_=fv[:, 2 * (i - 2) : 2 * (i - 1)])
        for h in range(2):
            nc.sync.dma_start(out=w_raw[h][:], in_=wv[:, :, h * (R // 2) : (h + 1) * (R // 2)])
        nc.sync.dma_start(out=wb_codes[:].bitcast(I32), in_=wb_words[0].bitcast(I32))
        for q in range(4):
            nc.sync.dma_start(
                out=wb_plane[32 * q : 32 * q + 4, :].bitcast(I32),
                in_=wb_scales[0, 4 * q : 4 * q + 4, :].bitcast(I32),
            )
        nc.sync.dma_start(out=resid[:], in_=rs.rearrange("(c p) j -> p c j", p=P))

        larger = [keep.tile([P, J], F32, name="larger%d" % i) for i in range(PACK)]
        pick_a = [keep.tile([P, J], F32, name="pick_a%d" % i) for i in range(PACK)]
        pick_b = [keep.tile([P, J], F32, name="pick_b%d" % i) for i in range(PACK)]

        def gather(i):
            nc.scalar.activation(pick_a[i][:], x_rows[i][:].indirect(list_a[:]), ACT.Copy)
            nc.vector.tensor_copy(pick_b[i][:], x_rows[i][:].indirect(list_b[:]))

        def keep_larger(i):
            nc.vector.tensor_tensor(larger[i][:], pick_a[i][:], pick_b[i][:], ALU.max)

        early = keep.tile([P, PACK - 1, J], BF16, name="early")

        def scale(i, dest):
            nc.vector.tensor_scalar(dest, larger[i][:], factor[i // 2][:, i % 2 : i % 2 + 1], None, ALU.mult)

        for i in range(2):
            gather(i)
            keep_larger(i)
        gather(2)
        scale(0, early[:, 0, :])
        scale(1, early[:, 1, :])
        keep_larger(2)
        gather(3)
        scale(2, early[:, 2, :])
        keep_larger(3)
        u_bf = keep.tile([P, J, PACK], BF16, name="u_bf", tag="x3", align_bytes=64)
        nc.vector.tensor_copy(u_bf[:, :, 0 : PACK - 1], early[:].rearrange("p i j -> p j i"))
        scale(3, u_bf[:, :, 3])

        u_codes = keep.tile([P, J], U32, name="u_codes", align_bytes=64)
        u_plane = keep.tile([P, J], U8, name="u_plane", align_bytes=64)
        nc.vector.quantize_mx(
            out=u_codes[:].bitcast(E4M3), scales=u_plane[:], in_=u_bf[:].rearrange("p j i -> p (j i)")
        )

        w_codes = keep.tile([P, R], U32, name="w_codes", align_bytes=64)
        w_plane = keep.tile([P, R], U8, name="w_plane", align_bytes=64)
        w_bf = [keep.tile([P, PACK, HALF_M, PACK], BF16, name="w_bf%d" % h, align_bytes=64) for h in range(2)]
        for h in range(2):
            dealt = w_bf[h][:].rearrange("p t m i -> p m t i")
            source = w_raw[h][:].rearrange("p i (m t) -> p m t i", t=PACK)
            cut = SCALAR_SHARE[h]
            nc.scalar.copy(dealt[:, 0:cut], source[:, 0:cut])
            if cut < HALF_M:
                nc.vector.tensor_copy(dealt[:, cut:HALF_M], source[:, cut:HALF_M])
        for h in range(2):
            for t in range(PACK):
                cols = slice(t * P + h * HALF_M, t * P + (h + 1) * HALF_M)
                nc.vector.quantize_mx(
                    out=w_codes[:, cols].bitcast(E5M2),
                    scales=w_plane[:, cols],
                    in_=w_bf[h][:, t].rearrange("p m i -> p (m i)"),
                )

        first = [psum.tile([P, PACK, HALF_J], F32, name="first%d" % s) for s in range(2)]
        for s in range(2):
            slots = slice(s * HALF_J, (s + 1) * HALF_J)
            for t in range(PACK):
                cols = slice(t * P, (t + 1) * P)
                nc.tensor.matmul_mx(
                    out=first[s][:, t, :],
                    lhsT=w_codes[:, cols].bitcast(E5M2),
                    lhsT_scale=w_plane[:, cols],
                    rhs=u_codes[:, slots].bitcast(E4M3),
                    rhs_scale=u_plane[:, slots],
                    start=True,
                    stop=True,
                )

        hid_bf = [keep.tile([P, PACK * HALF_J], BF16, name="hid_bf%d" % s, align_bytes=64) for s in range(2)]
        hid_codes = [keep.tile([P, HALF_J], U32, name="hid_codes%d" % s, align_bytes=64) for s in range(2)]
        hid_plane = [keep.tile([P, HALF_J], U8, name="hid_plane%d" % s, align_bytes=64) for s in range(2)]
        second = [[psum.tile([P, HALF_J], F32, name="second%d%d" % (s, c)) for c in range(2)] for s in range(2)]
        quarter = HALF_J // 2

        def hidden(s, e):
            j0 = s * HALF_J + e * quarter
            now = relu[:, PACK * (LAG + j0) : PACK * (LAG + j0 + quarter)]
            before = relu[:, PACK * j0 : PACK * (j0 + quarter)]
            nc.scalar.activation(
                now.rearrange("p (j t) -> p j t", t=PACK),
                first[s][:, :, e * quarter : (e + 1) * quarter].rearrange("p t j -> p j t"),
                ACT.Relu,
            )
            nc.vector.scalar_tensor_tensor(
                hid_bf[s][:, PACK * e * quarter : PACK * (e + 1) * quarter], before, -0.5, now, ALU.mult, ALU.add
            )

        def second_product(s):
            nc.vector.quantize_mx(out=hid_codes[s][:].bitcast(E5M2), scales=hid_plane[s][:], in_=hid_bf[s][:])
            for c in range(2):
                nc.tensor.matmul_mx(
                    out=second[s][c][:],
                    lhsT=wb_codes[:, 2 * P * c : 2 * P * (c + 1)].bitcast(E2M1),
                    lhsT_scale=wb_plane[:, P * c : P * (c + 1)],
                    rhs=hid_codes[s][:].bitcast(E5M2),
                    rhs_scale=hid_plane[s][:],
                    start=True,
                    stop=True,
                )

        hidden(0, 0)
        hidden(0, 1)
        hidden(1, 0)
        second_product(0)
        hidden(1, 1)
        second_product(1)

        out_v = out.rearrange("(c p) j -> p c j", p=P)
        for s in range(2):
            j0 = s * HALF_J
            lagged = min(HALF_J, J - 1 - j0)
            result = [keep.tile([P, HALF_J], F32, name="result%d%d" % (s, c)) for c in range(2)]
            for c in range(2):
                nc.vector.scalar_tensor_tensor(
                    resid[:, c, j0 + 1 : j0 + 1 + lagged],
                    second[s][c][:, 0:lagged],
                    -1.4,
                    resid[:, c, j0 + 1 : j0 + 1 + lagged],
                    ALU.mult,
                    ALU.add,
                )
            for c in range(2):
                nc.vector.scalar_tensor_tensor(
                    result[c][:], resid[:, c, j0 : j0 + HALF_J], 0.5, second[s][c][:], ALU.mult, ALU.add
                )
                queue = nc.sync if c == 0 else nc.scalar
                queue.dma_start(out=out_v[:, c, j0 : j0 + HALF_J], in_=result[c][:])
